import numpy as np
import ml_dtypes


def mxq(x, axis, fmt="e4m3"):
    dtype, down = {"e4m3": (ml_dtypes.float8_e4m3fn, 7), "e5m2": (ml_dtypes.float8_e5m2, 14)}[fmt]
    v = np.moveaxis(np.asarray(x, np.float32).astype(ml_dtypes.bfloat16).astype(np.float64), axis, -1)
    blocks = v.reshape(v.shape[:-1] + (-1, 32))
    amax = np.abs(blocks).max(-1, keepdims=True)
    byte = np.maximum(np.where(amax > 0, np.frexp(amax)[1] - 1 + 127, 0) - down, 1)
    scale = np.exp2(byte - 127.0)
    codes = (blocks / scale).astype(np.float32).astype(dtype).astype(np.float64)
    return np.moveaxis((codes * scale).reshape(v.shape), -1, axis)


WIDE = False


def mx_kscale(k):
    if not WIDE:
        return np.ones(k)
    levels = np.array([10, -10, 5, -5, 0])
    if k % 512:
        return np.exp2(np.random.permutation(np.resize(levels, k // 32))).repeat(32)
    a = np.empty((k // 512, 16))
    for p in range(k // 512):
        a[p, :8] = np.random.permutation(np.resize(levels, 8))
        for g in range(8):
            far = levels[np.abs(levels - a[p, g]) >= 10]
            a[p, g + 8] = far[np.random.randint(len(far))]
    return np.exp2(a.ravel()).repeat(32)


def f64(x):
    return np.asarray(x).astype(np.float64)


def striped(idx):
    return np.tile(idx.reshape(-1, 16).T, (8, 1)).astype(np.uint16)


def unstriped(offs):
    return offs[:16].T.reshape(-1).astype(np.int64)


E2M1 = np.array([0.0, 0.5, 1.0, 1.5, 2.0, 3.0, 4.0, 6.0, -0.0, -0.5, -1.0, -1.5, -2.0, -3.0, -4.0, -6.0])


def pack_weight(w, fmt):
    k, n = w.shape
    w = f64(np.asarray(w, np.float32).astype(ml_dtypes.bfloat16)).reshape(k // 32, 32, n)
    amax = np.abs(w).max(1)
    if fmt == "e4m3":
        byte = np.frexp(amax)[1] - 1 + 127 - 7
    else:
        mant, ex = np.frexp(amax / 6.0)
        byte = np.where(mant > 0.5, ex, ex - 1) + 127
    byte = np.clip(np.where(amax > 0, byte, 1), 1, 254)
    scaled = (w * np.exp2(127.0 - byte)[:, None, :]).reshape(k, n).astype(np.float32)
    by_word = np.ascontiguousarray(scaled.reshape(k // 512, 128, 4, n).transpose(0, 1, 3, 2))
    if fmt == "e4m3":
        words = by_word.astype(ml_dtypes.float8_e4m3fn).view(np.uint8)
    else:
        c = by_word.astype(ml_dtypes.float4_e2m1fn).view(np.uint8) & 0xF
        words = (c[..., 0::2] | (c[..., 1::2] << 4)).reshape(k // 512, 128, 2 * n)
    return np.ascontiguousarray(words), np.ascontiguousarray(byte.astype(np.uint8).reshape(k // 512, 16, n))


def unpack_weight(words, scales, fmt):
    g, _, n = scales.shape
    words = np.ascontiguousarray(words).reshape(g, 128, n, -1)
    if fmt == "e4m3":
        vals = words.view(ml_dtypes.float8_e4m3fn).astype(np.float64)
    else:
        nib = np.empty((g, 128, n, 4), np.uint8)
        nib[..., 0::2] = words & 0xF
        nib[..., 1::2] = words >> 4
        vals = E2M1[nib]
    vals = vals * np.repeat(np.exp2(scales.astype(np.float64) - 127.0), 8, axis=1)[..., None]
    return vals.transpose(0, 1, 3, 2).reshape(g * 512, n)


def silu(v):
    return v / (1.0 + np.exp(-np.maximum(v, -700.0)))


K, M, T, S = 512, 256, 2048, 1024


def setup_inputs():
    n = np.random.standard_normal
    s = mx_kscale(K)[:, None]
    s2 = mx_kscale(512)[:, None]
    v = pack_weight(n((K, T)) * s, "e4m3")
    p_w4 = pack_weight(n((K, M)) / np.sqrt(K) / s, "e2m1")
    return {
        "tab_words": v[0],
        "tab_scales": v[1],
        "w4_words": p_w4[0],
        "w4_scales": p_w4[1],
        "c": (n((512, S)) * s2).astype(np.float32),
        "u": (n((512, M)) / np.sqrt(512) / s2).astype(np.float32),
        "rT": n((M, T)).astype(np.float32),
        "b": (0.3 * n(256)).astype(np.float32),
        "offs": striped(np.random.permutation(T)[:S]),
    }


def reference(tab_words, tab_scales, w4_words, w4_scales, c, u, rT, b, offs):
    tab_ = unpack_weight(tab_words, tab_scales, "e4m3")[:, unstriped(offs)]
    w4_ = unpack_weight(w4_words, w4_scales, "e2m1")
    c_ = mxq(f64(c), 0, "e4m3")
    u_ = mxq(f64(u), 0, "e4m3")
    y = w4_.T @ tab_ + u_.T @ c_
    return (silu(y + f64(b)[:, None])) + f64(rT)[:, unstriped(offs)]

@@ -1,0 +1,156 @@
+from contextlib import ExitStack
+
+import concourse.mybir as mybir
+
+K, M, T, S = 512, 256, 2048, 1024
+FLOPS = 2 * 2 * K * M * S
+
+F32 = mybir.dt.float32
+BF16 = mybir.dt.bfloat16
+I32 = mybir.dt.int32
+U32 = mybir.dt.uint32
+U16 = mybir.dt.uint16
+U8 = mybir.dt.uint8
+FP8X4 = mybir.dt.float8_e4m3fn_x4
+FP4X4 = mybir.dt.float4_e2m1fn_x4
+SILU = mybir.ActivationFunctionType.Silu
+ADD = mybir.AluOpType.add
+
+P = 128
+PACK = 4
+HALVES = M // P
+WIDTHS = [256, 256, 256, 128, 128]
+FP4_N = 128
+PER_COL = 16
+
+
+def tile_list_tabres_silu_kernel(tc, tab_words, tab_scales, w4_words, w4_scales, c, u, rT, b, offs, out):
+    nc = tc.nc
+    starts = [sum(WIDTHS[:j]) for j in range(len(WIDTHS))]
+    chunks = [slice(s, s + w) for s, w in zip(starts, WIDTHS)]
+    last = len(chunks) - 1
+    with ExitStack() as ctx:
+        keep = ctx.enter_context(tc.tile_pool(name="keep", bufs=1))
+        psum = ctx.enter_context(tc.psum_pool(name="psum", bufs=1))
+
+        def load_scale_rows(queue, plane, rows):
+            for q in range(4):
+                queue.dma_start(plane[32 * q : 32 * q + 4, :].bitcast(I32), rows[4 * q : 4 * q + 4, :].bitcast(I32))
+
+        def interleave(copy, grouped, raw):
+            copy(grouped.rearrange("p (g i) t -> p g t i", i=4), raw.rearrange("p t (g i) -> p g t i", i=4))
+
+        offsets = keep.tile([P, S // PER_COL], U16, name="offsets")
+        tab_plane = keep.tile([P, T], U8, name="tab_plane", align_bytes=64)
+        w4_plane = keep.tile([P, M], U8, name="w4_plane", align_bytes=64)
+        tab = keep.tile([P, T], I32, name="tab", align_bytes=64)
+        res = [keep.tile([P, T], F32, name="res%d" % h, align_bytes=64) for h in range(HALVES)]
+        c_raw = [keep.tile([P, PACK, w], F32, name="c_raw%d" % j, align_bytes=64) for j, w in enumerate(WIDTHS)]
+        u_raw = keep.tile([P, PACK, M], F32, name="u_raw", align_bytes=64)
+        w4 = keep.tile([P, 2 * M], U8, name="w4", align_bytes=64)
+        bias = keep.tile([P, HALVES], F32, name="bias")
+        c_rows = c.rearrange("(p t) j -> p t j", t=PACK)
+
+        def load_tab(queue):
+            queue.dma_start(tab[:], tab_words[0].rearrange("p t i -> p (t i)").bitcast(I32))
+
+        def load_res(queue, h):
+            queue.dma_start(res[h][:], rT[P * h : P * (h + 1), :])
+
+        def load_u(queue):
+            queue.dma_start(u_raw[:], u.rearrange("(p t) n -> p t n", t=PACK))
+
+        def load_w4(queue):
+            queue.dma_start(w4[:].bitcast(I32), w4_words[0].bitcast(I32))
+
+        def load_bias(queue):
+            with nc.allow_non_contiguous_dma(reason="one bias value for each partition and half"):
+                queue.dma_start(bias[:], b.rearrange("(h p) -> p h", p=P))
+
+        def load_c(queue, j):
+            queue.dma_start(c_raw[j][:], c_rows[:, :, chunks[j]])
+
+        nc.sync.dma_start(offsets[:], offs)
+        nc.vector.memset(tab_plane[:].bitcast(I32), 0)
+        load_tab(nc.sync)
+        load_scale_rows(nc.sync, tab_plane, tab_scales[0])
+        load_res(nc.sync, 0)
+        load_u(nc.sync)
+        warm = keep.tile([P, 2], F32, name="warm")
+        nc.gpsimd.memset(warm[:, 0:1], 0.0)
+        nc.scalar.activation(warm[:, 1:2], warm[:, 0:1], SILU)
+        load_w4(nc.sync)
+        load_c(nc.sync, 0)
+        load_scale_rows(nc.sync, w4_plane, w4_scales[0])
+        load_res(nc.sync, 1)
+        load_bias(nc.sync)
+        for j in range(1, last + 1):
+            load_c(nc.sync, j)
+
+        v_plane = keep.tile([P, S], U8, name="v_plane", align_bytes=64)
+        nc.vector.tensor_copy(v_plane[:], tab_plane[:].indirect(offsets[:]))
+        v_codes = keep.tile([P, S], U32, name="v_codes", align_bytes=64)
+        nc.vector.tensor_copy(v_codes[:], tab[:].bitcast(U32).indirect(offsets[:]))
+        picked = [keep.tile([P, S], F32, name="picked%d" % h, align_bytes=64) for h in range(HALVES)]
+        nc.vector.tensor_copy(picked[0][:], res[0][:].indirect(offsets[:]))
+
+        u_grouped = keep.tile([P, M, PACK], BF16, name="u_grouped", align_bytes=64)
+        interleave(nc.scalar.copy, u_grouped[:], u_raw[:])
+        u_codes = keep.tile([P, M], U32, name="u_codes", align_bytes=64)
+        u_plane = keep.tile([P, M], U8, name="u_plane", align_bytes=64)
+        nc.vector.quantize_mx(u_codes[:].bitcast(FP8X4), u_plane[:], u_grouped[:].rearrange("p n t -> p (n t)"))
+
+        acc = {}
+        act = {}
+
+        def table_product(j):
+            for h in range(HALVES):
+                acc[h, j] = psum.tile([P, 512], F32, name="acc%d_%d" % (h, j % 4))
+                for n0 in range(0, WIDTHS[j], FP4_N):
+                    cols = slice(starts[j] + n0, starts[j] + n0 + FP4_N)
+                    nc.tensor.matmul_mx(
+                        acc[h, j][:, n0 : n0 + FP4_N],
+                        lhsT=w4[:, 2 * P * h : 2 * P * (h + 1)].bitcast(FP4X4),
+                        lhsT_scale=w4_plane[:, P * h : P * (h + 1)],
+                        rhs=v_codes[:, cols].bitcast(FP8X4),
+                        rhs_scale=v_plane[:, cols],
+                        start=(n0 == 0),
+                        stop=False,
+                    )
+
+        def feature_product(j):
+            width = WIDTHS[j]
+            c_grouped = keep.tile([P, width, PACK], BF16, name="c_grouped%d" % j, tag="ring%d" % j, align_bytes=64)
+            interleave(nc.vector.tensor_copy if j in () else nc.scalar.copy, c_grouped[:], c_raw[j][:])
+            c_codes = keep.tile([P, width], U32, name="c_codes%d" % j, align_bytes=64)
+            c_plane = keep.tile([P, width], U8, name="c_plane%d" % j, align_bytes=64)
+            nc.vector.quantize_mx(c_codes[:].bitcast(FP8X4), c_plane[:], c_grouped[:].rearrange("p n t -> p (n t)"))
+            for h in range(HALVES):
+                nc.tensor.matmul_mx(
+                    acc[h, j][:, 0:width],
+                    lhsT=u_codes[:, P * h : P * (h + 1)].bitcast(FP8X4),
+                    lhsT_scale=u_plane[:, P * h : P * (h + 1)],
+                    rhs=c_codes[:].bitcast(FP8X4),
+                    rhs_scale=c_plane[:],
+                    start=False,
+                    stop=True,
+                )
+                act[h, j] = keep.tile([P, width], F32, name="act%d_%d" % (h, j), align_bytes=64)
+                nc.scalar.activation(act[h, j][:], acc[h, j][:, 0:width], SILU, bias=bias[:, h : h + 1])
+
+        def finish(j):
+            total = keep.tile([P, HALVES, WIDTHS[j]], F32, name="total%d" % j, tag="ring%d" % min(j + 1, last + 1), align_bytes=64)
+            for h in range(HALVES):
+                nc.vector.tensor_tensor(total[:, h, :], picked[h][:, chunks[j]], act[h, j][:], ADD)
+                nc.sync.dma_start(out[P * h : P * (h + 1), chunks[j]], total[:, h, :])
+
+        for j in range(min(4, last + 1)):
+            table_product(j)
+        feature_product(0)
+        nc.vector.tensor_copy(picked[1][:], res[1][:].indirect(offsets[:]))
+        for j in range(1, last + 1):
+            if j >= 4:
+                table_product(j)
+            feature_product(j)
+            finish(j - 1)
+        finish(last)

@@ -19,16 +19,14 @@ ADD = mybir.AluOpType.add
 P = 128
 PACK = 4
 HALVES = M // P
-WIDTHS = [256, 256, 256, 128, 128]
-FP4_N = 128
+BANK = 512
+BANKS = S // BANK
+CHUNK = 256
 PER_COL = 16
 
 
 def tile_list_tabres_silu_kernel(tc, tab_words, tab_scales, w4_words, w4_scales, c, u, rT, b, offs, out):
     nc = tc.nc
-    starts = [sum(WIDTHS[:j]) for j in range(len(WIDTHS))]
-    chunks = [slice(s, s + w) for s, w in zip(starts, WIDTHS)]
-    last = len(chunks) - 1
     with ExitStack() as ctx:
         keep = ctx.enter_context(tc.tile_pool(name="keep", bufs=1))
         psum = ctx.enter_context(tc.psum_pool(name="psum", bufs=1))
@@ -40,16 +38,20 @@ def tile_list_tabres_silu_kernel(tc, tab_words, tab_scales, w4_words, w4_scales,
         def interleave(copy, grouped, raw):
             copy(grouped.rearrange("p (g i) t -> p g t i", i=4), raw.rearrange("p t (g i) -> p g t i", i=4))
 
+        def entries(cols):
+            return offsets[:, cols.start // PER_COL : cols.stop // PER_COL]
+
         offsets = keep.tile([P, S // PER_COL], U16, name="offsets")
         tab_plane = keep.tile([P, T], U8, name="tab_plane", align_bytes=64)
         w4_plane = keep.tile([P, M], U8, name="w4_plane", align_bytes=64)
         tab = keep.tile([P, T], I32, name="tab", align_bytes=64)
         res = [keep.tile([P, T], F32, name="res%d" % h, align_bytes=64) for h in range(HALVES)]
-        c_raw = [keep.tile([P, PACK, w], F32, name="c_raw%d" % j, align_bytes=64) for j, w in enumerate(WIDTHS)]
+        c_raw = [keep.tile([P, PACK, BANK], F32, name="c_raw%d" % a, align_bytes=64) for a in range(BANKS)]
         u_raw = keep.tile([P, PACK, M], F32, name="u_raw", align_bytes=64)
         w4 = keep.tile([P, 2 * M], U8, name="w4", align_bytes=64)
         bias = keep.tile([P, HALVES], F32, name="bias")
         c_rows = c.rearrange("(p t) j -> p t j", t=PACK)
+        spans = [slice(a * BANK, (a + 1) * BANK) for a in range(BANKS)]
 
         def load_tab(queue):
             queue.dma_start(tab[:], tab_words[0].rearrange("p t i -> p (t i)").bitcast(I32))
@@ -67,32 +69,30 @@ def tile_list_tabres_silu_kernel(tc, tab_words, tab_scales, w4_words, w4_scales,
             with nc.allow_non_contiguous_dma(reason="one bias value for each partition and half"):
                 queue.dma_start(bias[:], b.rearrange("(h p) -> p h", p=P))
 
-        def load_c(queue, j):
-            queue.dma_start(c_raw[j][:], c_rows[:, :, chunks[j]])
+        def load_c(queue, a):
+            queue.dma_start(c_raw[a][:], c_rows[:, :, spans[a]])
 
         nc.sync.dma_start(offsets[:], offs)
         nc.vector.memset(tab_plane[:].bitcast(I32), 0)
         load_tab(nc.sync)
         load_scale_rows(nc.sync, tab_plane, tab_scales[0])
-        load_res(nc.sync, 0)
         load_u(nc.sync)
+        load_c(nc.sync, 0)
         warm = keep.tile([P, 2], F32, name="warm")
         nc.gpsimd.memset(warm[:, 0:1], 0.0)
         nc.scalar.activation(warm[:, 1:2], warm[:, 0:1], SILU)
         load_w4(nc.sync)
-        load_c(nc.sync, 0)
-        load_scale_rows(nc.sync, w4_plane, w4_scales[0])
-        load_res(nc.sync, 1)
         load_bias(nc.sync)
-        for j in range(1, last + 1):
-            load_c(nc.sync, j)
+        load_scale_rows(nc.sync, w4_plane, w4_scales[0])
+        load_c(nc.sync, 1)
+        load_res(nc.sync, 0)
+        load_res(nc.sync, 1)
 
         v_plane = keep.tile([P, S], U8, name="v_plane", align_bytes=64)
-        nc.vector.tensor_copy(v_plane[:], tab_plane[:].indirect(offsets[:]))
         v_codes = keep.tile([P, S], U32, name="v_codes", align_bytes=64)
-        nc.vector.tensor_copy(v_codes[:], tab[:].bitcast(U32).indirect(offsets[:]))
-        picked = [keep.tile([P, S], F32, name="picked%d" % h, align_bytes=64) for h in range(HALVES)]
-        nc.vector.tensor_copy(picked[0][:], res[0][:].indirect(offsets[:]))
+        for cols in spans:
+            nc.vector.tensor_copy(v_codes[:, cols], tab[:].bitcast(U32).indirect(entries(cols)))
+            nc.vector.tensor_copy(v_plane[:, cols], tab_plane[:].indirect(entries(cols)))
 
         u_grouped = keep.tile([P, M, PACK], BF16, name="u_grouped", align_bytes=64)
         interleave(nc.scalar.copy, u_grouped[:], u_raw[:])
@@ -100,57 +100,45 @@ def tile_list_tabres_silu_kernel(tc, tab_words, tab_scales, w4_words, w4_scales,
         u_plane = keep.tile([P, M], U8, name="u_plane", align_bytes=64)
         nc.vector.quantize_mx(u_codes[:].bitcast(FP8X4), u_plane[:], u_grouped[:].rearrange("p n t -> p (n t)"))
 
-        acc = {}
-        act = {}
-
-        def table_product(j):
-            for h in range(HALVES):
-                acc[h, j] = psum.tile([P, 512], F32, name="acc%d_%d" % (h, j % 4))
-                for n0 in range(0, WIDTHS[j], FP4_N):
-                    cols = slice(starts[j] + n0, starts[j] + n0 + FP4_N)
-                    nc.tensor.matmul_mx(
-                        acc[h, j][:, n0 : n0 + FP4_N],
-                        lhsT=w4[:, 2 * P * h : 2 * P * (h + 1)].bitcast(FP4X4),
-                        lhsT_scale=w4_plane[:, P * h : P * (h + 1)],
-                        rhs=v_codes[:, cols].bitcast(FP8X4),
-                        rhs_scale=v_plane[:, cols],
-                        start=(n0 == 0),
-                        stop=False,
-                    )
-
-        def feature_product(j):
-            width = WIDTHS[j]
-            c_grouped = keep.tile([P, width, PACK], BF16, name="c_grouped%d" % j, tag="ring%d" % j, align_bytes=64)
-            interleave(nc.vector.tensor_copy if j in () else nc.scalar.copy, c_grouped[:], c_raw[j][:])
-            c_codes = keep.tile([P, width], U32, name="c_codes%d" % j, align_bytes=64)
-            c_plane = keep.tile([P, width], U8, name="c_plane%d" % j, align_bytes=64)
-            nc.vector.quantize_mx(c_codes[:].bitcast(FP8X4), c_plane[:], c_grouped[:].rearrange("p n t -> p (n t)"))
+        act = [keep.tile([P, S], F32, name="act%d" % h, align_bytes=64) for h in range(HALVES)]
+        for a in range(BANKS):
+            acc = [psum.tile([P, BANK], F32, name="acc%d_%d" % (h, a)) for h in range(HALVES)]
             for h in range(HALVES):
                 nc.tensor.matmul_mx(
-                    acc[h, j][:, 0:width],
-                    lhsT=u_codes[:, P * h : P * (h + 1)].bitcast(FP8X4),
-                    lhsT_scale=u_plane[:, P * h : P * (h + 1)],
-                    rhs=c_codes[:].bitcast(FP8X4),
-                    rhs_scale=c_plane[:],
-                    start=False,
-                    stop=True,
+                    acc[h][:],
+                    lhsT=w4[:, 2 * P * h : 2 * P * (h + 1)].bitcast(FP4X4),
+                    lhsT_scale=w4_plane[:, P * h : P * (h + 1)],
+                    rhs=v_codes[:, spans[a]].bitcast(FP8X4),
+                    rhs_scale=v_plane[:, spans[a]],
+                    start=True,
+                    stop=False,
                 )
-                act[h, j] = keep.tile([P, width], F32, name="act%d_%d" % (h, j), align_bytes=64)
-                nc.scalar.activation(act[h, j][:], acc[h, j][:, 0:width], SILU, bias=bias[:, h : h + 1])
-
-        def finish(j):
-            total = keep.tile([P, HALVES, WIDTHS[j]], F32, name="total%d" % j, tag="ring%d" % min(j + 1, last + 1), align_bytes=64)
+            firsts = range(0, BANK, CHUNK)
+            grouped = [keep.tile([P, CHUNK, PACK], BF16, name="c_grouped%d_%d" % (a, n0), align_bytes=64) for n0 in firsts]
+            for tile, n0 in zip(grouped, firsts):
+                interleave(nc.scalar.copy if a == 0 else nc.vector.tensor_copy, tile[:], c_raw[a][:, :, n0 : n0 + CHUNK])
+            for tile, n0 in zip(grouped, firsts):
+                c_codes = keep.tile([P, CHUNK], U32, name="c_codes%d_%d" % (a, n0), align_bytes=64)
+                c_plane = keep.tile([P, CHUNK], U8, name="c_plane%d_%d" % (a, n0), align_bytes=64)
+                nc.vector.quantize_mx(c_codes[:].bitcast(FP8X4), c_plane[:], tile[:].rearrange("p n t -> p (n t)"))
+                for h in range(HALVES):
+                    nc.tensor.matmul_mx(
+                        acc[h][:, n0 : n0 + CHUNK],
+                        lhsT=u_codes[:, P * h : P * (h + 1)].bitcast(FP8X4),
+                        lhsT_scale=u_plane[:, P * h : P * (h + 1)],
+                        rhs=c_codes[:].bitcast(FP8X4),
+                        rhs_scale=c_plane[:],
+                        start=False,
+                        stop=(n0 == firsts[-1]),
+                    )
             for h in range(HALVES):
-                nc.vector.tensor_tensor(total[:, h, :], picked[h][:, chunks[j]], act[h, j][:], ADD)
-                nc.sync.dma_start(out[P * h : P * (h + 1), chunks[j]], total[:, h, :])
+                nc.scalar.activation(act[h][:, spans[a]], acc[h][:], SILU, bias=bias[:, h : h + 1])
 
-        for j in range(min(4, last + 1)):
-            table_product(j)
-        feature_product(0)
-        nc.vector.tensor_copy(picked[1][:], res[1][:].indirect(offsets[:]))
-        for j in range(1, last + 1):
-            if j >= 4:
-                table_product(j)
-            feature_product(j)
-            finish(j - 1)
-        finish(last)
+        for h, widths in enumerate([[512, 512], [512, 256, 256]]):
+            first = 0
+            for width in widths:
+                cols = slice(first, first + width)
+                total = keep.tile([P, width], F32, name="total%d_%d" % (h, first), align_bytes=64)
+                nc.vector.tensor_tensor(total[:], res[h][:].indirect(entries(cols)), act[h][:, cols], ADD)
+                nc.sync.dma_start(out[P * h : P * (h + 1), cols], total[:])
+                first = first + width

@@ -32,8 +32,8 @@ def tile_list_tabres_silu_kernel(tc, tab_words, tab_scales, w4_words, w4_scales,
         psum = ctx.enter_context(tc.psum_pool(name="psum", bufs=1))
 
         def load_scale_rows(queue, plane, rows):
-            for q in range(4):
-                queue.dma_start(plane[32 * q : 32 * q + 4, :].bitcast(I32), rows[4 * q : 4 * q + 4, :].bitcast(I32))
+            for r in range(4):
+                queue.dma_start(plane[r:P:32, :].bitcast(I32), rows[r:16:4, :].bitcast(I32))
 
         def interleave(copy, grouped, raw):
             copy(grouped.rearrange("p (g i) t -> p g t i", i=4), raw.rearrange("p t (g i) -> p g t i", i=4))
@@ -46,10 +46,11 @@ def tile_list_tabres_silu_kernel(tc, tab_words, tab_scales, w4_words, w4_scales,
         w4_plane = keep.tile([P, M], U8, name="w4_plane", align_bytes=64)
         tab = keep.tile([P, T], I32, name="tab", align_bytes=64)
         res = [keep.tile([P, T], F32, name="res%d" % h, align_bytes=64) for h in range(HALVES)]
-        c_raw = [keep.tile([P, PACK, BANK], F32, name="c_raw%d" % a, align_bytes=64) for a in range(BANKS)]
+        c_raw = [keep.tile([P, PACK, BANK], F32, name="c_raw%d" % a, tag="span%d" % a, align_bytes=64) for a in range(BANKS)]
         u_raw = keep.tile([P, PACK, M], F32, name="u_raw", align_bytes=64)
         w4 = keep.tile([P, 2 * M], U8, name="w4", align_bytes=64)
-        bias = keep.tile([P, HALVES], F32, name="bias")
+        bias_rows = keep.tile([P, 32], F32, name="bias_rows", align_bytes=64)
+        bias = keep.tile([P, 32], F32, name="bias", align_bytes=64)
         c_rows = c.rearrange("(p t) j -> p t j", t=PACK)
         spans = [slice(a * BANK, (a + 1) * BANK) for a in range(BANKS)]
 
@@ -66,15 +67,15 @@ def tile_list_tabres_silu_kernel(tc, tab_words, tab_scales, w4_words, w4_scales,
             queue.dma_start(w4[:].bitcast(I32), w4_words[0].bitcast(I32))
 
         def load_bias(queue):
-            with nc.allow_non_contiguous_dma(reason="one bias value for each partition and half"):
-                queue.dma_start(bias[:], b.rearrange("(h p) -> p h", p=P))
+            nc.vector.memset(bias_rows[:], 0.0)
+            queue.dma_start(bias_rows[0:P:16, :], b.rearrange("(h q i) -> q h i", h=HALVES, i=32))
 
         def load_c(queue, a):
             queue.dma_start(c_raw[a][:], c_rows[:, :, spans[a]])
 
+        load_tab(nc.sync)
         nc.sync.dma_start(offsets[:], offs)
         nc.vector.memset(tab_plane[:].bitcast(I32), 0)
-        load_tab(nc.sync)
         load_scale_rows(nc.sync, tab_plane, tab_scales[0])
         load_u(nc.sync)
         load_c(nc.sync, 0)
@@ -94,18 +95,19 @@ def tile_list_tabres_silu_kernel(tc, tab_words, tab_scales, w4_words, w4_scales,
             nc.vector.tensor_copy(v_codes[:, cols], tab[:].bitcast(U32).indirect(entries(cols)))
             nc.vector.tensor_copy(v_plane[:, cols], tab_plane[:].indirect(entries(cols)))
 
+        nc.vector.transpose(bias[:], bias_rows[:])
         u_grouped = keep.tile([P, M, PACK], BF16, name="u_grouped", align_bytes=64)
         interleave(nc.scalar.copy, u_grouped[:], u_raw[:])
         u_codes = keep.tile([P, M], U32, name="u_codes", align_bytes=64)
         u_plane = keep.tile([P, M], U8, name="u_plane", align_bytes=64)
         nc.vector.quantize_mx(u_codes[:].bitcast(FP8X4), u_plane[:], u_grouped[:].rearrange("p n t -> p (n t)"))
 
-        act = [keep.tile([P, S], F32, name="act%d" % h, align_bytes=64) for h in range(HALVES)]
+        acc = {}
         for a in range(BANKS):
-            acc = [psum.tile([P, BANK], F32, name="acc%d_%d" % (h, a)) for h in range(HALVES)]
             for h in range(HALVES):
+                acc[h, a] = psum.tile([P, BANK], F32, name="acc%d_%d" % (h, a))
                 nc.tensor.matmul_mx(
-                    acc[h][:],
+                    acc[h, a][:],
                     lhsT=w4[:, 2 * P * h : 2 * P * (h + 1)].bitcast(FP4X4),
                     lhsT_scale=w4_plane[:, P * h : P * (h + 1)],
                     rhs=v_codes[:, spans[a]].bitcast(FP8X4),
@@ -116,14 +118,14 @@ def tile_list_tabres_silu_kernel(tc, tab_words, tab_scales, w4_words, w4_scales,
             firsts = range(0, BANK, CHUNK)
             grouped = [keep.tile([P, CHUNK, PACK], BF16, name="c_grouped%d_%d" % (a, n0), align_bytes=64) for n0 in firsts]
             for tile, n0 in zip(grouped, firsts):
-                interleave(nc.scalar.copy if a == 0 else nc.vector.tensor_copy, tile[:], c_raw[a][:, :, n0 : n0 + CHUNK])
+                interleave(nc.vector.tensor_copy if (a, n0) == (BANKS - 1, 0) else nc.scalar.copy, tile[:], c_raw[a][:, :, n0 : n0 + CHUNK])
             for tile, n0 in zip(grouped, firsts):
                 c_codes = keep.tile([P, CHUNK], U32, name="c_codes%d_%d" % (a, n0), align_bytes=64)
                 c_plane = keep.tile([P, CHUNK], U8, name="c_plane%d_%d" % (a, n0), align_bytes=64)
                 nc.vector.quantize_mx(c_codes[:].bitcast(FP8X4), c_plane[:], tile[:].rearrange("p n t -> p (n t)"))
                 for h in range(HALVES):
                     nc.tensor.matmul_mx(
-                        acc[h][:, n0 : n0 + CHUNK],
+                        acc[h, a][:, n0 : n0 + CHUNK],
                         lhsT=u_codes[:, P * h : P * (h + 1)].bitcast(FP8X4),
                         lhsT_scale=u_plane[:, P * h : P * (h + 1)],
                         rhs=c_codes[:].bitcast(FP8X4),
@@ -131,14 +133,18 @@ def tile_list_tabres_silu_kernel(tc, tab_words, tab_scales, w4_words, w4_scales,
                         start=False,
                         stop=(n0 == firsts[-1]),
                     )
+
+        act = []
+        for a in range(BANKS):
+            act.append(keep.tile([P, HALVES, BANK], F32, name="act%d" % a, tag="span%d" % (BANKS - 1 - a), align_bytes=64))
             for h in range(HALVES):
-                nc.scalar.activation(act[h][:, spans[a]], acc[h][:], SILU, bias=bias[:, h : h + 1])
+                nc.scalar.activation(act[a][:, h, :], acc[h, a][:], SILU, bias=bias[:, 16 * h : 16 * h + 1])
 
         for h, widths in enumerate([[512, 512], [512, 256, 256]]):
             first = 0
             for width in widths:
                 cols = slice(first, first + width)
                 total = keep.tile([P, width], F32, name="total%d_%d" % (h, first), align_bytes=64)
-                nc.vector.tensor_tensor(total[:], res[h][:].indirect(entries(cols)), act[h][:, cols], ADD)
+                nc.vector.tensor_tensor(total[:], res[h][:].indirect(entries(cols)), act[first // BANK][:, h, first % BANK : first % BANK + width], ADD)
                 nc.sync.dma_start(out[P * h : P * (h + 1), cols], total[:])
                 first = first + width

from contextlib import ExitStack

import concourse.mybir as mybir

K, M, T, S = 512, 256, 2048, 1024
FLOPS = 2 * 2 * K * M * S

F32 = mybir.dt.float32
BF16 = mybir.dt.bfloat16
I32 = mybir.dt.int32
U32 = mybir.dt.uint32
U16 = mybir.dt.uint16
U8 = mybir.dt.uint8
FP8X4 = mybir.dt.float8_e4m3fn_x4
FP4X4 = mybir.dt.float4_e2m1fn_x4
SILU = mybir.ActivationFunctionType.Silu
ADD = mybir.AluOpType.add

P = 128
PACK = 4
HALVES = M // P
BANK = 512
BANKS = S // BANK
CHUNK = 256
PER_COL = 16


def tile_list_tabres_silu_kernel(tc, tab_words, tab_scales, w4_words, w4_scales, c, u, rT, b, offs, out):
    nc = tc.nc
    with ExitStack() as ctx:
        keep = ctx.enter_context(tc.tile_pool(name="keep", bufs=1))
        psum = ctx.enter_context(tc.psum_pool(name="psum", bufs=1))

        def load_scale_rows(queue, plane, rows):
            for r in range(4):
                queue.dma_start(plane[r:P:32, :].bitcast(I32), rows[r:16:4, :].bitcast(I32))

        def interleave(copy, grouped, raw):
            copy(grouped.rearrange("p (g i) t -> p g t i", i=4), raw.rearrange("p t (g i) -> p g t i", i=4))

        def entries(cols):
            return offsets[:, cols.start // PER_COL : cols.stop // PER_COL]

        offsets = keep.tile([P, S // PER_COL], U16, name="offsets")
        tab_plane = keep.tile([P, T], U8, name="tab_plane", align_bytes=64)
        w4_plane = keep.tile([P, M], U8, name="w4_plane", align_bytes=64)
        tab = keep.tile([P, T], I32, name="tab", align_bytes=64)
        res = [keep.tile([P, T], F32, name="res%d" % h, align_bytes=64) for h in range(HALVES)]
        c_raw = [keep.tile([P, PACK, BANK], F32, name="c_raw%d" % a, tag="span%d" % a, align_bytes=64) for a in range(BANKS)]
        u_raw = keep.tile([P, PACK, M], F32, name="u_raw", align_bytes=64)
        w4 = keep.tile([P, 2 * M], U8, name="w4", align_bytes=64)
        bias_rows = keep.tile([P, 32], F32, name="bias_rows", align_bytes=64)
        bias = keep.tile([P, 32], F32, name="bias", align_bytes=64)
        c_rows = c.rearrange("(p t) j -> p t j", t=PACK)
        spans = [slice(a * BANK, (a + 1) * BANK) for a in range(BANKS)]

        def load_tab(queue):
            queue.dma_start(tab[:], tab_words[0].rearrange("p t i -> p (t i)").bitcast(I32))

        def load_res(queue, h):
            queue.dma_start(res[h][:], rT[P * h : P * (h + 1), :])

        def load_u(queue):
            queue.dma_start(u_raw[:], u.rearrange("(p t) n -> p t n", t=PACK))

        def load_w4(queue):
            queue.dma_start(w4[:].bitcast(I32), w4_words[0].bitcast(I32))

        def load_bias(queue):
            nc.vector.memset(bias_rows[:], 0.0)
            queue.dma_start(bias_rows[0:P:16, :], b.rearrange("(h q i) -> q h i", h=HALVES, i=32))

        def load_c(queue, a):
            queue.dma_start(c_raw[a][:], c_rows[:, :, spans[a]])

        load_tab(nc.sync)
        nc.sync.dma_start(offsets[:], offs)
        nc.vector.memset(tab_plane[:].bitcast(I32), 0)
        load_scale_rows(nc.sync, tab_plane, tab_scales[0])
        load_u(nc.sync)
        load_c(nc.sync, 0)
        warm = keep.tile([P, 2], F32, name="warm")
        nc.gpsimd.memset(warm[:, 0:1], 0.0)
        nc.scalar.activation(warm[:, 1:2], warm[:, 0:1], SILU)
        load_w4(nc.sync)
        load_bias(nc.sync)
        load_scale_rows(nc.sync, w4_plane, w4_scales[0])
        load_c(nc.sync, 1)
        load_res(nc.sync, 0)
        load_res(nc.sync, 1)

        v_plane = keep.tile([P, S], U8, name="v_plane", align_bytes=64)
        v_codes = keep.tile([P, S], U32, name="v_codes", align_bytes=64)
        for cols in spans:
            nc.vector.tensor_copy(v_codes[:, cols], tab[:].bitcast(U32).indirect(entries(cols)))
            nc.vector.tensor_copy(v_plane[:, cols], tab_plane[:].indirect(entries(cols)))

        nc.vector.transpose(bias[:], bias_rows[:])
        u_grouped = keep.tile([P, M, PACK], BF16, name="u_grouped", align_bytes=64)
        interleave(nc.scalar.copy, u_grouped[:], u_raw[:])
        u_codes = keep.tile([P, M], U32, name="u_codes", align_bytes=64)
        u_plane = keep.tile([P, M], U8, name="u_plane", align_bytes=64)
        nc.vector.quantize_mx(u_codes[:].bitcast(FP8X4), u_plane[:], u_grouped[:].rearrange("p n t -> p (n t)"))

        acc = {}
        for a in range(BANKS):
            for h in range(HALVES):
                acc[h, a] = psum.tile([P, BANK], F32, name="acc%d_%d" % (h, a))
                nc.tensor.matmul_mx(
                    acc[h, a][:],
                    lhsT=w4[:, 2 * P * h : 2 * P * (h + 1)].bitcast(FP4X4),
                    lhsT_scale=w4_plane[:, P * h : P * (h + 1)],
                    rhs=v_codes[:, spans[a]].bitcast(FP8X4),
                    rhs_scale=v_plane[:, spans[a]],
                    start=True,
                    stop=False,
                )
            firsts = range(0, BANK, CHUNK)
            grouped = [keep.tile([P, CHUNK, PACK], BF16, name="c_grouped%d_%d" % (a, n0), align_bytes=64) for n0 in firsts]
            for tile, n0 in zip(grouped, firsts):
                interleave(nc.vector.tensor_copy if (a, n0) == (BANKS - 1, 0) else nc.scalar.copy, tile[:], c_raw[a][:, :, n0 : n0 + CHUNK])
            for tile, n0 in zip(grouped, firsts):
                c_codes = keep.tile([P, CHUNK], U32, name="c_codes%d_%d" % (a, n0), align_bytes=64)
                c_plane = keep.tile([P, CHUNK], U8, name="c_plane%d_%d" % (a, n0), align_bytes=64)
                nc.vector.quantize_mx(c_codes[:].bitcast(FP8X4), c_plane[:], tile[:].rearrange("p n t -> p (n t)"))
                for h in range(HALVES):
                    nc.tensor.matmul_mx(
                        acc[h, a][:, n0 : n0 + CHUNK],
                        lhsT=u_codes[:, P * h : P * (h + 1)].bitcast(FP8X4),
                        lhsT_scale=u_plane[:, P * h : P * (h + 1)],
                        rhs=c_codes[:].bitcast(FP8X4),
                        rhs_scale=c_plane[:],
                        start=False,
                        stop=(n0 == firsts[-1]),
                    )

        act = []
        for a in range(BANKS):
            act.append(keep.tile([P, HALVES, BANK], F32, name="act%d" % a, tag="span%d" % (BANKS - 1 - a), align_bytes=64))
            for h in range(HALVES):
                nc.scalar.activation(act[a][:, h, :], acc[h, a][:], SILU, bias=bias[:, 16 * h : 16 * h + 1])

        for h, widths in enumerate([[512, 512], [512, 256, 256]]):
            first = 0
            for width in widths:
                cols = slice(first, first + width)
                total = keep.tile([P, width], F32, name="total%d_%d" % (h, first), align_bytes=64)
                nc.vector.tensor_tensor(total[:], res[h][:].indirect(entries(cols)), act[first // BANK][:, h, first % BANK : first % BANK + width], ADD)
                nc.sync.dma_start(out[P * h : P * (h + 1), cols], total[:])
                first = first + width
